import numpy as np
import ml_dtypes


def mxq(x, axis, fmt="e4m3"):
    dtype, down = {"e4m3": (ml_dtypes.float8_e4m3fn, 7), "e5m2": (ml_dtypes.float8_e5m2, 14)}[fmt]
    v = np.moveaxis(np.asarray(x, np.float32).astype(ml_dtypes.bfloat16).astype(np.float64), axis, -1)
    blocks = v.reshape(v.shape[:-1] + (-1, 32))
    amax = np.abs(blocks).max(-1, keepdims=True)
    byte = np.maximum(np.where(amax > 0, np.frexp(amax)[1] - 1 + 127, 0) - down, 1)
    scale = np.exp2(byte - 127.0)
    codes = (blocks / scale).astype(np.float32).astype(dtype).astype(np.float64)
    return np.moveaxis((codes * scale).reshape(v.shape), -1, axis)


WIDE = False


def mx_kscale(k):
    if not WIDE:
        return np.ones(k)
    levels = np.array([10, -10, 5, -5, 0])
    if k % 512:
        return np.exp2(np.random.permutation(np.resize(levels, k // 32))).repeat(32)
    a = np.empty((k // 512, 16))
    for p in range(k // 512):
        a[p, :8] = np.random.permutation(np.resize(levels, 8))
        for g in range(8):
            far = levels[np.abs(levels - a[p, g]) >= 10]
            a[p, g + 8] = far[np.random.randint(len(far))]
    return np.exp2(a.ravel()).repeat(32)


BF16 = ml_dtypes.bfloat16


def bf(x):
    return np.asarray(x, np.float32).astype(BF16)


def f64(x):
    return np.asarray(x).astype(np.float64)


E2M1 = np.array([0.0, 0.5, 1.0, 1.5, 2.0, 3.0, 4.0, 6.0, -0.0, -0.5, -1.0, -1.5, -2.0, -3.0, -4.0, -6.0])


def pack_weight(w, fmt):
    k, n = w.shape
    w = f64(bf(w)).reshape(k // 32, 32, n)
    amax = np.abs(w).max(1)
    if fmt == "e4m3":
        byte = np.frexp(amax)[1] - 1 + 127 - 7
    else:
        mant, ex = np.frexp(amax / 6.0)
        byte = np.where(mant > 0.5, ex, ex - 1) + 127
    byte = np.clip(np.where(amax > 0, byte, 1), 1, 254)
    scaled = (w * np.exp2(127.0 - byte)[:, None, :]).reshape(k, n).astype(np.float32)
    by_word = np.ascontiguousarray(scaled.reshape(k // 512, 128, 4, n).transpose(0, 1, 3, 2))
    if fmt == "e4m3":
        words = by_word.astype(ml_dtypes.float8_e4m3fn).view(np.uint8)
    else:
        c = by_word.astype(ml_dtypes.float4_e2m1fn).view(np.uint8) & 0xF
        words = c[..., 0::2] | (c[..., 1::2] << 4)
    return np.ascontiguousarray(words), np.ascontiguousarray(byte.astype(np.uint8).reshape(k // 512, 16, n))


def unpack_weight(words, scales, fmt):
    g, p, n, _ = words.shape
    if fmt == "e4m3":
        vals = np.ascontiguousarray(words).view(ml_dtypes.float8_e4m3fn).astype(np.float64)
    else:
        nib = np.empty((g, p, n, 4), np.uint8)
        nib[..., 0::2] = words & 0xF
        nib[..., 1::2] = words >> 4
        vals = E2M1[nib]
    vals = vals * np.repeat(np.exp2(scales.astype(np.float64) - 127.0), 8, axis=1)[..., None]
    return vals.transpose(0, 1, 3, 2).reshape(g * 512, n)
def pack4(w):
    words, scales = pack_weight(w, "e2m1")
    return words.reshape(words.shape[0], 128, -1), scales


def unpack4(words, scales):
    return unpack_weight(words.reshape(words.shape[0], 128, -1, 2), scales, "e2m1")


D, T, N = 768, 2048, 1024


def setup_inputs():
    s = mx_kscale(T)
    frames = np.random.standard_normal((D, T)) * s
    near = np.random.standard_normal((N, T)) / np.sqrt(T) / s
    mid = np.random.standard_normal((T, N)) / np.sqrt(T) / s[:, None]
    far = np.random.standard_normal((T, N)) / np.sqrt(T) / s[:, None]
    mid_words, mid_scales = pack_weight(mid, "e4m3")
    far_words, far_scales = pack4(far)
    return {"frames": bf(frames),
            "variance": bf(0.5 + 1.5 * np.random.random(T)),
            "near": bf(near),
            "mid_words": mid_words, "mid_scales": mid_scales,
            "far_words": far_words, "far_scales": far_scales,
            "decay_mid": bf(0.8 * (1 + 0.1 * np.random.standard_normal(N))),
            "decay_far": bf(0.6 * (1 + 0.1 * np.random.standard_normal(N)))}


def reference(frames, variance, near, mid_words, mid_scales, far_words, far_scales, decay_mid, decay_far):
    a = mxq(f64(frames) / f64(variance), 1, "e4m3")
    r_near = a @ mxq(f64(near), 1, "e4m3").T
    r_mid = a @ unpack_weight(mid_words, mid_scales, "e4m3")
    r_far = a @ unpack4(far_words, far_scales)
    return r_near + f64(decay_mid) * r_mid + f64(decay_far) * r_far

@@ -1,0 +1,344 @@
+from contextlib import ExitStack
+
+import concourse.mybir as mybir
+from concourse.masks import make_identity
+
+D, T, N = 768, 2048, 1024
+FLOPS = 3 * 2 * D * T * N
+
+F32 = mybir.dt.float32
+BF16 = mybir.dt.bfloat16
+I32 = mybir.dt.int32
+U32 = mybir.dt.uint32
+U8 = mybir.dt.uint8
+FP8X4 = mybir.dt.float8_e4m3fn_x4
+FP4X4 = mybir.dt.float4_e2m1fn_x4
+ALU = mybir.AluOpType
+
+P = 128
+G = T // 512
+ROW_TILES = D // P
+NEAR_TILES = N // P
+HALF = 512
+
+
+def tile_wpe_tied_tap_correlation_s10_kernel(
+    tc, frames, variance, near, mid_words, mid_scales, far_words, far_scales, decay_mid, decay_far, out
+):
+    nc = tc.nc
+    with ExitStack() as ctx:
+        keep = ctx.enter_context(tc.tile_pool(name="keep", bufs=1))
+        stage = ctx.enter_context(tc.tile_pool(name="stage", bufs=2))
+        psum = ctx.enter_context(tc.psum_pool(name="psum", bufs=1))
+        ctx.enter_context(tc.manual_schedule())
+
+        ident = keep.tile([P, P], F32, name="ident")
+        make_identity(nc, ident[:])
+
+        far_plane = keep.tile([P, G, N], U8, name="far_plane", align_bytes=64)
+        mid_plane = keep.tile([P, N], U8, name="mid_plane", align_bytes=64)
+        nc.vector.memset(far_plane[:].rearrange("p g n -> p (g n)").bitcast(I32), 0)
+        nc.vector.memset(mid_plane[:].bitcast(I32), 0)
+
+        var_sb = keep.tile([P, G, 4], BF16, name="var_sb")
+        inv_var = keep.tile([P, G, 4], F32, name="inv_var")
+        frames_raw = {}
+        near_raw = {}
+        far_codes = {}
+        mid_codes = {}
+        decay_raw = {}
+
+        def load_frames(i, parts):
+            width = T // parts
+            for c in range(parts):
+                raw = keep.tile([P, width], BF16, name="frames_%d_%d" % (i, c), align_bytes=64)
+                nc.sync.dma_start(out=raw[:], in_=frames[i * P : (i + 1) * P, c * width : (c + 1) * width])
+                for g in range(c * G // parts, (c + 1) * G // parts):
+                    off = g * 256 - c * width // 2
+                    frames_raw[i, g] = raw[:].bitcast(F32)[:, off : off + 256]
+                if parts == 1:
+                    frames_raw[i] = raw[:].bitcast(F32)
+
+        def load_near(n):
+            raw = keep.tile([P, T], BF16, name="near_%d" % n, align_bytes=64)
+            nc.sync.dma_start(out=raw[:], in_=near[n * P : (n + 1) * P, :])
+            near_raw[n] = raw[:].bitcast(F32)
+
+        def load_far(h):
+            codes = keep.tile([P, G, 2 * HALF], U8, name="far_%d" % h, align_bytes=64)
+            src = far_words.rearrange("g p n -> p g n")[:, :, 2 * HALF * h : 2 * HALF * (h + 1)]
+            nc.sync.dma_start(out=codes[:].bitcast(I32), in_=src.bitcast(I32))
+            far_codes[h] = codes
+
+        def load_mid(h):
+            codes = keep.tile([P, G, HALF], U32, name="mid_%d" % h, align_bytes=64)
+            src = mid_words.rearrange("g p n t -> p g (n t)")[:, :, 4 * HALF * h : 4 * HALF * (h + 1)]
+            nc.sync.dma_start(out=codes[:].bitcast(I32), in_=src.bitcast(I32))
+            mid_codes[h] = codes
+
+        def load_far_scales():
+            rows = far_scales.rearrange("g (q r) n -> r q g n", r=4)
+            for r in range(4):
+                nc.sync.dma_start(out=far_plane[r:P:32, :, :].bitcast(I32), in_=rows[r].bitcast(I32))
+
+        def load_mid_scales():
+            for q in range(4):
+                nc.sync.dma_start(
+                    out=mid_plane[32 * q : 32 * q + 16, :].bitcast(I32),
+                    in_=mid_scales[:, 4 * q : 4 * q + 4, :].bitcast(I32),
+                )
+
+        def load_decay(which, vec):
+            raw = keep.tile([P, 8], BF16, name="decay_raw_" + which)
+            nc.sync.dma_start(out=raw[:], in_=vec.rearrange("(p c) -> p c", p=P))
+            decay_raw[which] = raw
+
+        nc.sync.dma_start(out=var_sb[:], in_=variance.rearrange("(g p t) -> p g t", g=G, p=P))
+        load_frames(0, 2)
+        load_frames(1, 1)
+        load_far_scales()
+        load_decay("far", decay_far)
+        load_far(0)
+        load_far(1)
+        load_decay("mid", decay_mid)
+        load_frames(2, 1)
+        load_mid_scales()
+        load_mid(0)
+        load_frames(3, 1)
+        load_mid(1)
+        load_frames(4, 1)
+        load_near(0)
+        load_frames(5, 1)
+        for n in range(1, NEAR_TILES):
+            load_near(n)
+
+        nc.vector.reciprocal(out=inv_var[:], in_=var_sb[:])
+
+        counters = {"tp": 0, "acc": 0}
+
+        def bank(kind, shape):
+            idx = counters[kind] % 4
+            counters[kind] = counters[kind] + 1
+            return psum.tile(shape, F32, name="%s_%d" % (kind, counters[kind]), tag="%s%d" % (kind, idx))
+
+        sorted_words = {}
+
+        def presort(key, raw):
+            srt = stage.tile([P, G, 2, P], F32, name="sorted_%s_%d" % key, tag="sorted", bufs=4, align_bytes=64)
+            nc.scalar.copy(out=srt[:], in_=raw.rearrange("r (g p u) -> r g u p", g=G, u=2))
+            sorted_words[key] = srt
+
+        banks = {}
+
+        def transpose_tile(key):
+            for b in range(2):
+                tp = bank("tp", [P, 2, 2, P])
+                for gg in range(2):
+                    g = 2 * b + gg
+                    for u in range(2):
+                        if key in sorted_words:
+                            src = sorted_words[key][:, g, u, :]
+                        else:
+                            src = frames_raw[key[1], g][:, u:256:2]
+                        nc.tensor.transpose(tp[:, gg, u, :], src, ident[:])
+                banks[key, b] = tp
+
+        decay_b = {}
+
+        def spread_decay(which):
+            tp = bank("acc", [P, 4, P])
+            words = decay_raw[which][:].bitcast(F32)
+            for c in range(4):
+                nc.tensor.transpose(tp[:, c, :], words[:, c : c + 1].to_broadcast([P, P]), ident[:])
+            wide = keep.tile([P, N], BF16, name="decay_" + which, align_bytes=64)
+            nc.scalar.copy(
+                out=wide[:].bitcast(F32).rearrange("m (p c) -> m p c", c=4),
+                in_=tp[:].rearrange("m c p -> m p c"),
+            )
+            decay_b[which] = wide
+
+        a_grouped = {}
+        a_codes = {}
+        a_scales = {}
+
+        def divide(i, g):
+            if g == 0:
+                a_grouped[i] = stage.tile([P, G, P, 4], BF16, name="a_grouped_%d" % i, tag="a_grouped", align_bytes=64)
+                a_codes[i] = keep.tile([P, G, P], U32, name="a_codes_%d" % i, align_bytes=64)
+                a_scales[i] = keep.tile([P, G, P], U8, name="a_scales_%d" % i, align_bytes=64)
+            tp = banks[("f", i), g // 2]
+            pairs = tp[:].rearrange("p g u r -> p (g u r)").bitcast(BF16)
+            pairs = pairs.rearrange("p (g u r e) -> p g r u e", g=2, u=2, e=2)[:, g % 2]
+            nc.vector.tensor_tensor(
+                out=a_grouped[i][:, g].rearrange("p r (u e) -> p r u e", u=2),
+                in0=pairs,
+                in1=inv_var[:, g, :].rearrange("p (u e) -> p u e", u=2).unsqueeze(1).to_broadcast([P, P, 2, 2]),
+                op=ALU.mult,
+            )
+
+        def quantise_a(i, g0, g1):
+            nc.vector.quantize_mx(
+                out=a_codes[i][:, g0:g1, :].rearrange("p g r -> p (g r)").bitcast(FP8X4),
+                scales=a_scales[i][:, g0:g1, :].rearrange("p g r -> p (g r)"),
+                in_=a_grouped[i][:, g0:g1].rearrange("p g r t -> p (g r t)"),
+            )
+
+        near_grouped = {}
+        near_codes = {}
+        near_scales = {}
+        for h in range(2):
+            near_codes[h] = keep.tile([P, G, HALF], U32, name="near_codes_%d" % h, align_bytes=64)
+            near_scales[h] = keep.tile([P, G, HALF], U8, name="near_scales_%d" % h, align_bytes=64)
+
+        def interleave_near(n):
+            grouped = stage.tile([P, G, P, 4], BF16, name="n_grouped_%d" % n, tag="n_grouped", bufs=3, align_bytes=64)
+            words = grouped[:].rearrange("p g r t -> p (g r t)").bitcast(F32)
+            words = words.rearrange("p (g r u) -> p g r u", g=G, u=2)
+            for b in range(2):
+                nc.scalar.copy(
+                    out=words[:, 2 * b : 2 * b + 2],
+                    in_=banks[("n", n), b][:].rearrange("p g u r -> p g r u"),
+                )
+            near_grouped[n] = grouped
+
+        def quantise_near(n):
+            h, cols = n // 4, slice((n % 4) * P, (n % 4 + 1) * P)
+            for g in range(G):
+                nc.vector.quantize_mx(
+                    out=near_codes[h][:, g, cols].bitcast(FP8X4),
+                    scales=near_scales[h][:, g, cols],
+                    in_=near_grouped[n][:, g].rearrange("p r t -> p (r t)"),
+                )
+
+        accs = {}
+
+        def product(kind, i, h):
+            acc = bank("acc", [P, HALF])
+            cols = slice(h * HALF, (h + 1) * HALF)
+            for g in range(G):
+                if kind == "far":
+                    rhs, rhs_scale = far_codes[h][:, g, :].bitcast(FP4X4), far_plane[:, g, cols]
+                elif kind == "mid":
+                    rhs, rhs_scale = mid_codes[h][:, g, :].bitcast(FP8X4), mid_plane[4 * g : P, cols]
+                else:
+                    rhs, rhs_scale = near_codes[h][:, g, :].bitcast(FP8X4), near_scales[h][:, g, :]
+                nc.tensor.matmul_mx(
+                    out=acc[:],
+                    lhsT=a_codes[i][:, g, :].bitcast(FP8X4),
+                    lhsT_scale=a_scales[i][:, g, :],
+                    rhs=rhs,
+                    rhs_scale=rhs_scale,
+                    start=(g == 0),
+                    stop=(g == G - 1),
+                )
+            accs[kind, i, h] = acc
+
+        tied = {}
+
+        def weigh(kind, i, h):
+            part = keep.tile([P, HALF], F32, name="tied_%s_%d_%d" % (kind, i, h))
+            nc.vector.tensor_tensor(
+                out=part[:], in0=accs[kind, i, h][:], in1=decay_b[kind][:, h * HALF : (h + 1) * HALF], op=ALU.mult
+            )
+            tied[kind, i, h] = part
+
+        def join(i, h):
+            nc.vector.tensor_tensor(
+                out=tied["far", i, h][:], in0=tied["far", i, h][:], in1=tied["mid", i, h][:], op=ALU.add
+            )
+
+        def finish(i, h):
+            result = tied["mid", i, h]
+            nc.vector.tensor_tensor(out=result[:], in0=accs["near", i, h][:], in1=tied["far", i, h][:], op=ALU.add)
+            nc.sync.dma_start(out=out[i * P : (i + 1) * P, h * HALF : (h + 1) * HALF], in_=result[:])
+
+        transpose_tile(("f", 0))
+        transpose_tile(("f", 1))
+        spread_decay("far")
+        divide(0, 0)
+        for g in range(1, G):
+            divide(0, g)
+            quantise_a(0, g - 1, g)
+        divide(1, 0)
+        quantise_a(0, G - 1, G)
+        product("far", 0, 0)
+        product("far", 0, 1)
+        for g in range(1, G):
+            divide(1, g)
+        weigh("far", 0, 0)
+        quantise_a(1, 0, G)
+        transpose_tile(("f", 2))
+        spread_decay("mid")
+        weigh("far", 0, 1)
+        product("far", 1, 0)
+        product("far", 1, 1)
+        presort(("f", 3), frames_raw[3])
+        for g in range(G):
+            divide(2, g)
+        weigh("far", 1, 0)
+        quantise_a(2, 0, G)
+        weigh("far", 1, 1)
+        product("mid", 0, 0)
+        product("mid", 1, 0)
+        weigh("mid", 0, 0)
+        transpose_tile(("f", 3))
+        presort(("f", 4), frames_raw[4])
+        presort(("n", 0), near_raw[0])
+        weigh("mid", 1, 0)
+        product("mid", 0, 1)
+        product("mid", 1, 1)
+        for g in range(G):
+            divide(3, g)
+        weigh("mid", 0, 1)
+        quantise_a(3, 0, G)
+
+        runs = {
+            2: [("f", 4), ("n", 0)],
+            3: [("f", 5), ("n", 1)],
+            4: [("n", 2), ("n", 3)],
+            5: [("n", 4), ("n", 5)],
+            6: [("n", 6), ("n", 7)],
+            7: [],
+        }
+        joins = [(i, h) for i in range(ROW_TILES) for h in range(2)]
+        for i in range(2, ROW_TILES):
+            for key in runs[i]:
+                transpose_tile(key)
+            weigh("mid", i - 1, 1)
+            for kind, n in runs[i]:
+                if kind == "n":
+                    interleave_near(n)
+            for kind, n in runs[i + 1]:
+                presort((kind, n), frames_raw[n] if kind == "f" else near_raw[n])
+            product("far", i, 0)
+            product("far", i, 1)
+            product("mid", i, 0)
+            first_kind, first = runs[i][0]
+            if first_kind == "f":
+                for g in range(G):
+                    divide(first, g)
+                weigh("far", i, 0)
+                quantise_a(first, 0, G)
+            else:
+                for k in range(4):
+                    join(*joins[4 * (i - 4) + k])
+                weigh("far", i, 0)
+                quantise_near(first)
+            weigh("far", i, 1)
+            quantise_near(runs[i][1][1])
+            product("mid", i, 1)
+            weigh("mid", i, 0)
+
+        for key in runs[6]:
+            transpose_tile(key)
+        weigh("mid", ROW_TILES - 1, 1)
+        interleave_near(6)
+        interleave_near(7)
+        order = [(i, h) for h in range(2) for i in range(ROW_TILES)]
+        extra = [lambda: join(4, 0), lambda: quantise_near(6), lambda: quantise_near(7), lambda: join(5, 0),
+                 lambda: join(4, 1), lambda: join(5, 1)]
+        for k, (i, h) in enumerate(order):
+            product("near", i, h)
+            if k < len(extra):
+                extra[k]()
+            finish(i, h)

@@ -37,8 +37,13 @@ def tile_wpe_tied_tap_correlation_s10_kernel(
 
         far_plane = keep.tile([P, G, N], U8, name="far_plane", align_bytes=64)
         mid_plane = keep.tile([P, N], U8, name="mid_plane", align_bytes=64)
-        nc.vector.memset(far_plane[:].rearrange("p g n -> p (g n)").bitcast(I32), 0)
+        warm_in = keep.tile([P, 4 * P], BF16, name="warm_in", align_bytes=64)
+        warm_codes = keep.tile([P, P], U32, name="warm_codes", align_bytes=64)
+        warm_scales = keep.tile([P, P], U8, name="warm_scales", align_bytes=64)
+        nc.vector.memset(warm_in[:], 0.0)
         nc.vector.memset(mid_plane[:].bitcast(I32), 0)
+        nc.vector.quantize_mx(out=warm_codes[:].bitcast(FP8X4), scales=warm_scales[:], in_=warm_in[:])
+        nc.vector.memset(far_plane[:].rearrange("p g n -> p (g n)").bitcast(I32), 0)
 
         var_sb = keep.tile([P, G, 4], BF16, name="var_sb")
         inv_var = keep.tile([P, G, 4], F32, name="inv_var")
@@ -64,11 +69,11 @@ def tile_wpe_tied_tap_correlation_s10_kernel(
             nc.sync.dma_start(out=raw[:], in_=near[n * P : (n + 1) * P, :])
             near_raw[n] = raw[:].bitcast(F32)
 
-        def load_far(h):
-            codes = keep.tile([P, G, 2 * HALF], U8, name="far_%d" % h, align_bytes=64)
-            src = far_words.rearrange("g p n -> p g n")[:, :, 2 * HALF * h : 2 * HALF * (h + 1)]
+        def load_far(pair):
+            codes = keep.tile([P, 2, 2 * N], U8, name="far_%d" % pair, align_bytes=64)
+            src = far_words.rearrange("g p n -> p g n")[:, 2 * pair : 2 * pair + 2, :]
             nc.sync.dma_start(out=codes[:].bitcast(I32), in_=src.bitcast(I32))
-            far_codes[h] = codes
+            far_codes[pair] = codes
 
         def load_mid(h):
             codes = keep.tile([P, G, HALF], U32, name="mid_%d" % h, align_bytes=64)
@@ -93,14 +98,17 @@ def tile_wpe_tied_tap_correlation_s10_kernel(
             nc.sync.dma_start(out=raw[:], in_=vec.rearrange("(p c) -> p c", p=P))
             decay_raw[which] = raw
 
-        nc.sync.dma_start(out=var_sb[:], in_=variance.rearrange("(g p t) -> p g t", g=G, p=P))
+        def load_variance():
+            nc.sync.dma_start(out=var_sb[:], in_=variance.rearrange("(g p t) -> p g t", g=G, p=P))
+
+        load_variance()
         load_frames(0, 2)
         load_frames(1, 1)
-        load_far_scales()
         load_decay("far", decay_far)
+        load_decay("mid", decay_mid)
+        load_far_scales()
         load_far(0)
         load_far(1)
-        load_decay("mid", decay_mid)
         load_frames(2, 1)
         load_mid_scales()
         load_mid(0)
@@ -140,7 +148,7 @@ def tile_wpe_tied_tap_correlation_s10_kernel(
                             src = sorted_words[key][:, g, u, :]
                         else:
                             src = frames_raw[key[1], g][:, u:256:2]
-                        nc.tensor.transpose(tp[:, gg, u, :], src, ident[:])
+                        nc.tensor.transpose(tp[:, u, gg, :], src, ident[:])
                 banks[key, b] = tp
 
         decay_b = {}
@@ -161,18 +169,20 @@ def tile_wpe_tied_tap_correlation_s10_kernel(
         a_codes = {}
         a_scales = {}
 
-        def divide(i, g):
+        def divide(i, g, g1=None):
+            g1 = g + 1 if g1 is None else g1
             if g == 0:
                 a_grouped[i] = stage.tile([P, G, P, 4], BF16, name="a_grouped_%d" % i, tag="a_grouped", align_bytes=64)
                 a_codes[i] = keep.tile([P, G, P], U32, name="a_codes_%d" % i, align_bytes=64)
                 a_scales[i] = keep.tile([P, G, P], U8, name="a_scales_%d" % i, align_bytes=64)
             tp = banks[("f", i), g // 2]
-            pairs = tp[:].rearrange("p g u r -> p (g u r)").bitcast(BF16)
-            pairs = pairs.rearrange("p (g u r e) -> p g r u e", g=2, u=2, e=2)[:, g % 2]
+            pairs = tp[:].rearrange("p u g r -> p (u g r)").bitcast(BF16)
+            pairs = pairs.rearrange("p (u g r e) -> p g r u e", g=2, u=2, e=2)[:, g % 2 : g % 2 + g1 - g]
+            factors = inv_var[:, g:g1, :].rearrange("p g (u e) -> p g u e", u=2).unsqueeze(2)
             nc.vector.tensor_tensor(
-                out=a_grouped[i][:, g].rearrange("p r (u e) -> p r u e", u=2),
+                out=a_grouped[i][:, g:g1].rearrange("p g r (u e) -> p g r u e", u=2),
                 in0=pairs,
-                in1=inv_var[:, g, :].rearrange("p (u e) -> p u e", u=2).unsqueeze(1).to_broadcast([P, P, 2, 2]),
+                in1=factors.to_broadcast([P, g1 - g, P, 2, 2]),
                 op=ALU.mult,
             )
 
@@ -197,7 +207,7 @@ def tile_wpe_tied_tap_correlation_s10_kernel(
             for b in range(2):
                 nc.scalar.copy(
                     out=words[:, 2 * b : 2 * b + 2],
-                    in_=banks[("n", n), b][:].rearrange("p g u r -> p g r u"),
+                    in_=banks[("n", n), b][:].rearrange("p u g r -> p g r u"),
                 )
             near_grouped[n] = grouped
 
@@ -212,16 +222,22 @@ def tile_wpe_tied_tap_correlation_s10_kernel(
 
         accs = {}
 
-        def product(kind, i, h):
-            acc = bank("acc", [P, HALF])
+        def product(kind, i, h, g0=0, g1=G, part=None):
+            lo, width = (0, HALF) if part is None else (part * HALF // 2, HALF // 2)
+            key = (kind, i, h) if part is None else (kind, i, h, part)
+            if g0 == 0:
+                accs[key] = bank("acc", [P, width])
+            acc = accs[key]
             cols = slice(h * HALF, (h + 1) * HALF)
-            for g in range(G):
+            for g in range(g0, g1):
                 if kind == "far":
-                    rhs, rhs_scale = far_codes[h][:, g, :].bitcast(FP4X4), far_plane[:, g, cols]
+                    words = far_codes[g // 2][:, g % 2, 2 * h * HALF : 2 * (h + 1) * HALF]
+                    rhs, rhs_scale = words.bitcast(FP4X4), far_plane[:, g, cols]
                 elif kind == "mid":
                     rhs, rhs_scale = mid_codes[h][:, g, :].bitcast(FP8X4), mid_plane[4 * g : P, cols]
                 else:
-                    rhs, rhs_scale = near_codes[h][:, g, :].bitcast(FP8X4), near_scales[h][:, g, :]
+                    rhs = near_codes[h][:, g, lo : lo + width].bitcast(FP8X4)
+                    rhs_scale = near_scales[h][:, g, lo : lo + width]
                 nc.tensor.matmul_mx(
                     out=acc[:],
                     lhsT=a_codes[i][:, g, :].bitcast(FP8X4),
@@ -231,7 +247,20 @@ def tile_wpe_tied_tap_correlation_s10_kernel(
                     start=(g == 0),
                     stop=(g == G - 1),
                 )
-            accs[kind, i, h] = acc
+
+        warm_bank = bank("acc", [P, 4, P])
+
+        def warm_up(count):
+            for k in range(count):
+                nc.tensor.matmul_mx(
+                    out=warm_bank[:, k % 4, :],
+                    lhsT=warm_codes[:].bitcast(FP8X4),
+                    lhsT_scale=warm_scales[:],
+                    rhs=warm_codes[:].bitcast(FP8X4),
+                    rhs_scale=warm_scales[:],
+                    start=True,
+                    stop=True,
+                )
 
         tied = {}
 
@@ -247,34 +276,39 @@ def tile_wpe_tied_tap_correlation_s10_kernel(
                 out=tied["far", i, h][:], in0=tied["far", i, h][:], in1=tied["mid", i, h][:], op=ALU.add
             )
 
-        def finish(i, h):
-            result = tied["mid", i, h]
-            nc.vector.tensor_tensor(out=result[:], in0=accs["near", i, h][:], in1=tied["far", i, h][:], op=ALU.add)
-            nc.sync.dma_start(out=out[i * P : (i + 1) * P, h * HALF : (h + 1) * HALF], in_=result[:])
+        def finish(i, h, part=None):
+            lo, width = (0, HALF) if part is None else (part * HALF // 2, HALF // 2)
+            key = ("near", i, h) if part is None else ("near", i, h, part)
+            result = tied["mid", i, h][:, lo : lo + width]
+            nc.vector.tensor_tensor(out=result, in0=accs[key][:], in1=tied["far", i, h][:, lo : lo + width], op=ALU.add)
+            nc.sync.dma_start(out=out[i * P : (i + 1) * P, h * HALF + lo : h * HALF + lo + width], in_=result)
 
+        warm_up(15)
         transpose_tile(("f", 0))
+        warm_up(18)
+        presort(("f", 1), frames_raw[1])
         transpose_tile(("f", 1))
         spread_decay("far")
+        spread_decay("mid")
         divide(0, 0)
         for g in range(1, G):
             divide(0, g)
             quantise_a(0, g - 1, g)
-        divide(1, 0)
+        divide(1, 0, 2)
         quantise_a(0, G - 1, G)
-        product("far", 0, 0)
-        product("far", 0, 1)
-        for g in range(1, G):
-            divide(1, g)
-        weigh("far", 0, 0)
-        quantise_a(1, 0, G)
+        for g0 in (0, 2):
+            product("far", 0, 0, g0, g0 + 2)
+            product("far", 0, 1, g0, g0 + 2)
+        divide(1, 2, 4)
         transpose_tile(("f", 2))
-        spread_decay("mid")
+        quantise_a(1, 0, G)
+        weigh("far", 0, 0)
         weigh("far", 0, 1)
         product("far", 1, 0)
         product("far", 1, 1)
         presort(("f", 3), frames_raw[3])
-        for g in range(G):
-            divide(2, g)
+        divide(2, 0, 2)
+        divide(2, 2, 4)
         weigh("far", 1, 0)
         quantise_a(2, 0, G)
         weigh("far", 1, 1)
@@ -287,8 +321,8 @@ def tile_wpe_tied_tap_correlation_s10_kernel(
         weigh("mid", 1, 0)
         product("mid", 0, 1)
         product("mid", 1, 1)
-        for g in range(G):
-            divide(3, g)
+        divide(3, 0, 2)
+        divide(3, 2, 4)
         weigh("mid", 0, 1)
         quantise_a(3, 0, G)
 
@@ -315,8 +349,8 @@ def tile_wpe_tied_tap_correlation_s10_kernel(
             product("mid", i, 0)
             first_kind, first = runs[i][0]
             if first_kind == "f":
-                for g in range(G):
-                    divide(first, g)
+                divide(first, 0, 2)
+                divide(first, 2, 4)
                 weigh("far", i, 0)
                 quantise_a(first, 0, G)
             else:
@@ -337,8 +371,12 @@ def tile_wpe_tied_tap_correlation_s10_kernel(
         order = [(i, h) for h in range(2) for i in range(ROW_TILES)]
         extra = [lambda: join(4, 0), lambda: quantise_near(6), lambda: quantise_near(7), lambda: join(5, 0),
                  lambda: join(4, 1), lambda: join(5, 1)]
-        for k, (i, h) in enumerate(order):
+        for k, (i, h) in enumerate(order[:-1]):
             product("near", i, h)
             if k < len(extra):
                 extra[k]()
             finish(i, h)
+        for part in range(2):
+            product("near", ROW_TILES - 1, 1, part=part)
+        for part in range(2):
+            finish(ROW_TILES - 1, 1, part)

@@ -20,6 +20,7 @@ G = T // 512
 ROW_TILES = D // P
 NEAR_TILES = N // P
 HALF = 512
+LAST_PARTS = [(0, 256), (256, 128), (384, 128)]
 
 
 def tile_wpe_tied_tap_correlation_s10_kernel(
@@ -133,7 +134,10 @@ def tile_wpe_tied_tap_correlation_s10_kernel(
 
         def presort(key, raw):
             srt = stage.tile([P, G, 2, P], F32, name="sorted_%s_%d" % key, tag="sorted", bufs=4, align_bytes=64)
-            nc.scalar.copy(out=srt[:], in_=raw.rearrange("r (g p u) -> r g u p", g=G, u=2))
+            nc.scalar.copy(
+                out=srt[:].rearrange("r g u (c i) -> r g c u i", i=4),
+                in_=raw.rearrange("r (g c i u) -> r g c u i", g=G, i=4, u=2),
+            )
             sorted_words[key] = srt
 
         banks = {}
@@ -223,7 +227,7 @@ def tile_wpe_tied_tap_correlation_s10_kernel(
         accs = {}
 
         def product(kind, i, h, g0=0, g1=G, part=None):
-            lo, width = (0, HALF) if part is None else (part * HALF // 2, HALF // 2)
+            lo, width = (0, HALF) if part is None else LAST_PARTS[part]
             key = (kind, i, h) if part is None else (kind, i, h, part)
             if g0 == 0:
                 accs[key] = bank("acc", [P, width])
@@ -270,14 +274,16 @@ def tile_wpe_tied_tap_correlation_s10_kernel(
                 out=part[:], in0=accs[kind, i, h][:], in1=decay_b[kind][:, h * HALF : (h + 1) * HALF], op=ALU.mult
             )
             tied[kind, i, h] = part
+            if kind == "mid":
+                join(i, h)
 
         def join(i, h):
-            nc.vector.tensor_tensor(
+            nc.gpsimd.tensor_tensor(
                 out=tied["far", i, h][:], in0=tied["far", i, h][:], in1=tied["mid", i, h][:], op=ALU.add
             )
 
         def finish(i, h, part=None):
-            lo, width = (0, HALF) if part is None else (part * HALF // 2, HALF // 2)
+            lo, width = (0, HALF) if part is None else LAST_PARTS[part]
             key = ("near", i, h) if part is None else ("near", i, h, part)
             result = tied["mid", i, h][:, lo : lo + width]
             nc.vector.tensor_tensor(out=result, in0=accs[key][:], in1=tied["far", i, h][:, lo : lo + width], op=ALU.add)
@@ -334,7 +340,6 @@ def tile_wpe_tied_tap_correlation_s10_kernel(
             6: [("n", 6), ("n", 7)],
             7: [],
         }
-        joins = [(i, h) for i in range(ROW_TILES) for h in range(2)]
         for i in range(2, ROW_TILES):
             for key in runs[i]:
                 transpose_tile(key)
@@ -354,8 +359,6 @@ def tile_wpe_tied_tap_correlation_s10_kernel(
                 weigh("far", i, 0)
                 quantise_a(first, 0, G)
             else:
-                for k in range(4):
-                    join(*joins[4 * (i - 4) + k])
                 weigh("far", i, 0)
                 quantise_near(first)
             weigh("far", i, 1)
@@ -369,14 +372,12 @@ def tile_wpe_tied_tap_correlation_s10_kernel(
         interleave_near(6)
         interleave_near(7)
         order = [(i, h) for h in range(2) for i in range(ROW_TILES)]
-        extra = [lambda: join(4, 0), lambda: quantise_near(6), lambda: quantise_near(7), lambda: join(5, 0),
-                 lambda: join(4, 1), lambda: join(5, 1)]
         for k, (i, h) in enumerate(order[:-1]):
             product("near", i, h)
-            if k < len(extra):
-                extra[k]()
             finish(i, h)
-        for part in range(2):
+            if k < 2:
+                quantise_near(6 + k)
+        for part in range(len(LAST_PARTS)):
             product("near", ROW_TILES - 1, 1, part=part)
-        for part in range(2):
+        for part in range(len(LAST_PARTS)):
             finish(ROW_TILES - 1, 1, part)

@@ -48,33 +48,36 @@ def tile_wpe_tied_tap_correlation_s10_kernel(
 
         var_sb = keep.tile([P, G, 4], BF16, name="var_sb")
         inv_var = keep.tile([P, G, 4], F32, name="inv_var")
-        frames_raw = {}
-        near_raw = {}
+        raw_words = {}
+        quadrant_words = {}
         far_codes = {}
         mid_codes = {}
         decay_raw = {}
 
-        def load_frames(i, parts):
+        def load_frames(i, parts, only=None):
             width = T // parts
-            for c in range(parts):
+            for c in range(parts) if only is None else [only]:
                 raw = keep.tile([P, width], BF16, name="frames_%d_%d" % (i, c), align_bytes=64)
                 nc.sync.dma_start(out=raw[:], in_=frames[i * P : (i + 1) * P, c * width : (c + 1) * width])
-                for g in range(c * G // parts, (c + 1) * G // parts):
-                    off = g * 256 - c * width // 2
-                    frames_raw[i, g] = raw[:].bitcast(F32)[:, off : off + 256]
-                if parts == 1:
-                    frames_raw[i] = raw[:].bitcast(F32)
+                raw_words["f", i, c] = raw[:].bitcast(F32)
 
         def load_near(n):
             raw = keep.tile([P, T], BF16, name="near_%d" % n, align_bytes=64)
             nc.sync.dma_start(out=raw[:], in_=near[n * P : (n + 1) * P, :])
-            near_raw[n] = raw[:].bitcast(F32)
+            raw_words["n", n, 0] = raw[:].bitcast(F32)
 
-        def load_far(pair):
-            codes = keep.tile([P, 2, 2 * N], U8, name="far_%d" % pair, align_bytes=64)
-            src = far_words.rearrange("g p n -> p g n")[:, 2 * pair : 2 * pair + 2, :]
-            nc.sync.dma_start(out=codes[:].bitcast(I32), in_=src.bitcast(I32))
-            far_codes[pair] = codes
+        def load_near_by_quadrant(b):
+            raw = keep.tile([P, 2, 8, P], BF16, name="near_last_%d" % b, align_bytes=64)
+            rows = near[N - 2 * P :, :].rearrange("(s r) (g q k) -> g q r s k", r=32, g=G, q=4)
+            for gg in range(2):
+                for q in (0, 2, 1, 3):
+                    nc.sync.dma_start(out=raw[32 * q : 32 * (q + 1), gg], in_=rows[2 * b + gg, q])
+            quadrant_words[b] = raw[:].rearrange("r g s k -> r (g s k)").bitcast(F32)
+
+        def load_far(g):
+            codes = keep.tile([P, 2 * N], U8, name="far_%d" % g, align_bytes=64)
+            nc.sync.dma_start(out=codes[:].bitcast(I32), in_=far_words[g].bitcast(I32))
+            far_codes[g] = codes
 
         def load_mid(h):
             codes = keep.tile([P, G, HALF], U32, name="mid_%d" % h, align_bytes=64)
@@ -82,10 +85,11 @@ def tile_wpe_tied_tap_correlation_s10_kernel(
             nc.sync.dma_start(out=codes[:].bitcast(I32), in_=src.bitcast(I32))
             mid_codes[h] = codes
 
-        def load_far_scales():
+        def load_far_scales(which, queue):
             rows = far_scales.rearrange("g (q r) n -> r q g n", r=4)
-            for r in range(4):
-                nc.sync.dma_start(out=far_plane[r:P:32, :, :].bitcast(I32), in_=rows[r].bitcast(I32))
+            engine = nc.sync if queue == "sync" else nc.gpsimd
+            for r in which:
+                engine.dma_start(out=far_plane[r:P:32, :, :].bitcast(I32), in_=rows[r].bitcast(I32))
 
         def load_mid_scales():
             for q in range(4):
@@ -103,57 +107,75 @@ def tile_wpe_tied_tap_correlation_s10_kernel(
             nc.sync.dma_start(out=var_sb[:], in_=variance.rearrange("(g p t) -> p g t", g=G, p=P))
 
         load_variance()
-        load_frames(0, 2)
-        load_frames(1, 1)
+        load_frames(0, 2, 0)
         load_decay("far", decay_far)
         load_decay("mid", decay_mid)
-        load_far_scales()
-        load_far(0)
-        load_far(1)
-        load_frames(2, 1)
+        load_frames(0, 2, 1)
+        load_frames(1, 2)
+        load_far_scales((0, 1, 2, 3), "sync")
+        for g in range(G):
+            load_far(g)
+        load_frames(2, 2)
+        for i in range(3, ROW_TILES):
+            load_frames(i, 1)
+        load_near(0)
+        load_near(1)
         load_mid_scales()
         load_mid(0)
-        load_frames(3, 1)
+        load_near(2)
+        load_near(3)
+        load_near(4)
+        load_near_by_quadrant(0)
+        load_near(5)
+        load_near_by_quadrant(1)
         load_mid(1)
-        load_frames(4, 1)
-        load_near(0)
-        load_frames(5, 1)
-        for n in range(1, NEAR_TILES):
-            load_near(n)
 
         nc.vector.reciprocal(out=inv_var[:], in_=var_sb[:])
 
-        counters = {"tp": 0, "acc": 0}
+        rings = {"tp": ["tp0", "tp1", "tp2", "tp3"], "acc": ["acc0", "acc1", "acc2", "acc3"]}
+        taken = []
 
         def bank(kind, shape):
-            idx = counters[kind] % 4
-            counters[kind] = counters[kind] + 1
-            return psum.tile(shape, F32, name="%s_%d" % (kind, counters[kind]), tag="%s%d" % (kind, idx))
+            tag = rings[kind][0]
+            rings[kind] = rings[kind][1:] + [tag]
+            taken.append(tag)
+            return psum.tile(shape, F32, name="bank_%d" % len(taken), tag=tag)
+
+        def widen_ring():
+            rings["acc"] = rings["acc"] + rings["tp"]
 
         sorted_words = {}
 
-        def presort(key, raw):
-            srt = stage.tile([P, G, 2, P], F32, name="sorted_%s_%d" % key, tag="sorted", bufs=4, align_bytes=64)
+        def presort(key, half=None):
+            passes = G if half is None else G // 2
+            raw = raw_words[key[0], key[1], 0 if half is None else half]
+            if half is None:
+                srt = stage.tile([P, G, 2, P], F32, name="sorted_%s_%d" % key, tag="sorted", bufs=5, align_bytes=64)
+            else:
+                srt = keep.tile([P, passes, 2, P], F32, name="sorted_%s_%d_%d" % (key + (half,)), align_bytes=64)
             nc.scalar.copy(
                 out=srt[:].rearrange("r g u (c i) -> r g c u i", i=4),
-                in_=raw.rearrange("r (g c i u) -> r g c u i", g=G, i=4, u=2),
+                in_=raw.rearrange("r (g c i u) -> r g c u i", g=passes, i=4, u=2),
             )
-            sorted_words[key] = srt
+            for g in range(passes):
+                sorted_words[key, g + (0 if half is None else passes * half)] = srt[:, g]
 
         banks = {}
 
+        def transpose_bank(key, b):
+            tp = bank("tp", [P, 2, 2, P])
+            for gg in range(2):
+                for u in range(2):
+                    if (key, 2 * b + gg) in sorted_words:
+                        src = sorted_words[key, 2 * b + gg][:, u, :]
+                    else:
+                        src = raw_words[key[0], key[1], b][:, 256 * gg + u : 256 * (gg + 1) : 2]
+                    nc.tensor.transpose(tp[:, u, gg, :], src, ident[:])
+            banks[key, b] = tp
+
         def transpose_tile(key):
             for b in range(2):
-                tp = bank("tp", [P, 2, 2, P])
-                for gg in range(2):
-                    g = 2 * b + gg
-                    for u in range(2):
-                        if key in sorted_words:
-                            src = sorted_words[key][:, g, u, :]
-                        else:
-                            src = frames_raw[key[1], g][:, u:256:2]
-                        nc.tensor.transpose(tp[:, u, gg, :], src, ident[:])
-                banks[key, b] = tp
+                transpose_bank(key, b)
 
         decay_b = {}
 
@@ -162,10 +184,13 @@ def tile_wpe_tied_tap_correlation_s10_kernel(
             words = decay_raw[which][:].bitcast(F32)
             for c in range(4):
                 nc.tensor.transpose(tp[:, c, :], words[:, c : c + 1].to_broadcast([P, P]), ident[:])
+            banks["decay", which] = tp
+
+        def keep_decay(which):
             wide = keep.tile([P, N], BF16, name="decay_" + which, align_bytes=64)
             nc.scalar.copy(
                 out=wide[:].bitcast(F32).rearrange("m (p c) -> m p c", c=4),
-                in_=tp[:].rearrange("m c p -> m p c"),
+                in_=banks["decay", which][:].rearrange("m c p -> m p c"),
             )
             decay_b[which] = wide
 
@@ -204,24 +229,53 @@ def tile_wpe_tied_tap_correlation_s10_kernel(
             near_codes[h] = keep.tile([P, G, HALF], U32, name="near_codes_%d" % h, align_bytes=64)
             near_scales[h] = keep.tile([P, G, HALF], U8, name="near_scales_%d" % h, align_bytes=64)
 
-        def interleave_near(n):
-            grouped = stage.tile([P, G, P, 4], BF16, name="n_grouped_%d" % n, tag="n_grouped", bufs=3, align_bytes=64)
-            words = grouped[:].rearrange("p g r t -> p (g r t)").bitcast(F32)
-            words = words.rearrange("p (g r u) -> p g r u", g=G, u=2)
-            for b in range(2):
-                nc.scalar.copy(
-                    out=words[:, 2 * b : 2 * b + 2],
-                    in_=banks[("n", n), b][:].rearrange("p u g r -> p g r u"),
+        def interleave_near(n, b, engine="scalar"):
+            if n % 2 == 0 and b == 0:
+                near_grouped[n // 2] = stage.tile(
+                    [P, G, 2 * P, 4], BF16, name="n_grouped_%d" % (n // 2), tag="n_grouped", align_bytes=64
                 )
-            near_grouped[n] = grouped
+            words = near_grouped[n // 2][:].rearrange("p g r t -> p (g r t)").bitcast(F32)
+            words = words.rearrange("p (g r u) -> p g r u", g=G, u=2)
+            dst = words[:, 2 * b : 2 * b + 2, (n % 2) * P : (n % 2 + 1) * P]
+            src = banks[("n", n), b][:].rearrange("p u g r -> p g r u")
+            if engine == "scalar":
+                nc.scalar.copy(out=dst, in_=src)
+            else:
+                nc.vector.tensor_copy(out=dst, in_=src)
 
-        def quantise_near(n):
-            h, cols = n // 4, slice((n % 4) * P, (n % 4 + 1) * P)
+        turned = {}
+
+        def presort_quadrants(b):
+            srt = stage.tile([P, 16, 2, 32], F32, name="sorted_last_%d" % b, tag="sorted", bufs=5, align_bytes=64)
+            nc.scalar.copy(
+                out=srt[:].rearrange("r s u (c i) -> r s c u i", i=4),
+                in_=quadrant_words[b].rearrange("r (s c i u) -> r s c u i", s=16, i=4, u=2),
+            )
+            sorted_words["last", b] = srt
+
+        def turn_quadrants(b):
+            turned[b] = keep.tile([P, 16, 2, 32], F32, name="turned_%d" % b, align_bytes=64)
+            nc.vector.transpose(
+                out=turned[b][:].rearrange("p s u r -> p (s u r)"),
+                in_=sorted_words["last", b][:].rearrange("r s u j -> r (s u j)"),
+            )
+
+        def interleave_turned(b):
+            if b == 0:
+                near_grouped[3] = stage.tile([P, G, 2 * P, 4], BF16, name="n_grouped_3", tag="n_grouped", align_bytes=64)
+            words = near_grouped[3][:, 2 * b : 2 * b + 2].rearrange("p g r t -> p (g r t)").bitcast(F32)
+            nc.scalar.copy(
+                out=words.rearrange("p (s r u) -> p s r u", s=16, u=2),
+                in_=turned[b][:].rearrange("p s u r -> p s r u"),
+            )
+
+        def quantise_near(pair):
+            h, cols = pair // 2, slice((pair % 2) * 2 * P, (pair % 2 + 1) * 2 * P)
             for g in range(G):
                 nc.vector.quantize_mx(
                     out=near_codes[h][:, g, cols].bitcast(FP8X4),
                     scales=near_scales[h][:, g, cols],
-                    in_=near_grouped[n][:, g].rearrange("p r t -> p (r t)"),
+                    in_=near_grouped[pair][:, g].rearrange("p r t -> p (r t)"),
                 )
 
         accs = {}
@@ -235,7 +289,7 @@ def tile_wpe_tied_tap_correlation_s10_kernel(
             cols = slice(h * HALF, (h + 1) * HALF)
             for g in range(g0, g1):
                 if kind == "far":
-                    words = far_codes[g // 2][:, g % 2, 2 * h * HALF : 2 * (h + 1) * HALF]
+                    words = far_codes[g][:, 2 * h * HALF : 2 * (h + 1) * HALF]
                     rhs, rhs_scale = words.bitcast(FP4X4), far_plane[:, g, cols]
                 elif kind == "mid":
                     rhs, rhs_scale = mid_codes[h][:, g, :].bitcast(FP8X4), mid_plane[4 * g : P, cols]
@@ -274,8 +328,17 @@ def tile_wpe_tied_tap_correlation_s10_kernel(
                 out=part[:], in0=accs[kind, i, h][:], in1=decay_b[kind][:, h * HALF : (h + 1) * HALF], op=ALU.mult
             )
             tied[kind, i, h] = part
-            if kind == "mid":
-                join(i, h)
+
+        def park(i, h):
+            part = keep.tile([P, HALF], F32, name="tied_far_%d_%d" % (i, h))
+            nc.scalar.copy(out=part[:], in_=accs["far", i, h][:])
+            tied["far", i, h] = part
+
+        def weigh_parked(i, h):
+            part = tied["far", i, h]
+            nc.vector.tensor_tensor(
+                out=part[:], in0=part[:], in1=decay_b["far"][:, h * HALF : (h + 1) * HALF], op=ALU.mult
+            )
 
         def join(i, h):
             nc.gpsimd.tensor_tensor(
@@ -291,92 +354,113 @@ def tile_wpe_tied_tap_correlation_s10_kernel(
 
         warm_up(15)
         transpose_tile(("f", 0))
-        warm_up(18)
-        presort(("f", 1), frames_raw[1])
-        transpose_tile(("f", 1))
+        warm_up(12)
         spread_decay("far")
         spread_decay("mid")
-        divide(0, 0)
-        for g in range(1, G):
-            divide(0, g)
-            quantise_a(0, g - 1, g)
-        divide(1, 0, 2)
-        quantise_a(0, G - 1, G)
-        for g0 in (0, 2):
-            product("far", 0, 0, g0, g0 + 2)
-            product("far", 0, 1, g0, g0 + 2)
-        divide(1, 2, 4)
-        transpose_tile(("f", 2))
-        quantise_a(1, 0, G)
-        weigh("far", 0, 0)
-        weigh("far", 0, 1)
-        product("far", 1, 0)
-        product("far", 1, 1)
-        presort(("f", 3), frames_raw[3])
-        divide(2, 0, 2)
-        divide(2, 2, 4)
-        weigh("far", 1, 0)
-        quantise_a(2, 0, G)
-        weigh("far", 1, 1)
-        product("mid", 0, 0)
-        product("mid", 1, 0)
+        for b in range(2):
+            presort(("f", 1), b)
+            transpose_bank(("f", 1), b)
+        keep_decay("far")
+        keep_decay("mid")
+        for b in range(2):
+            presort(("f", 2), b)
+        early = [(i, g) for i in range(2) for g in range(G)]
+        divide(0, 0, 1)
+        for k, (i, g) in enumerate(early):
+            if k + 1 < len(early):
+                divide(early[k + 1][0], early[k + 1][1], early[k + 1][1] + 1)
+            quantise_a(i, g, g + 1)
+            if (i, g) == (1, 1):
+                transpose_tile(("f", 2))
+            for h in range(2):
+                product("far", i, h, g, g + 1)
+        park(0, 0)
+        presort(("f", 3))
+        park(0, 1)
+
+        runs = {2: [3], 3: [4, 5], 4: []}
+        upcoming = {2: [], 3: [("n", 0)], 4: [("n", 1), ("n", 2)]}
+        for i in range(2, ROW_TILES - 1):
+            divide(i, 0, 2)
+            divide(i, 2, 4)
+            quantise_a(i, 0, 2)
+            quantise_a(i, 2, 4)
+            for n in runs[i]:
+                transpose_tile(("f", n))
+            if i == 2:
+                presort(("f", 4))
+                presort(("f", 5))
+            for h in range(2):
+                park(i - 1, h)
+            for key in upcoming[i]:
+                presort(key)
+            if i == 4:
+                product("mid", 0, 0)
+            for h in range(2):
+                product("far", i, h)
+        last = ROW_TILES - 1
+        divide(last, 0, 2)
+        divide(last, 2, 4)
+        quantise_a(last, 0, 2)
+        quantise_a(last, 2, 4)
         weigh("mid", 0, 0)
-        transpose_tile(("f", 3))
-        presort(("f", 4), frames_raw[4])
-        presort(("n", 0), near_raw[0])
-        weigh("mid", 1, 0)
-        product("mid", 0, 1)
-        product("mid", 1, 1)
-        divide(3, 0, 2)
-        divide(3, 2, 4)
-        weigh("mid", 0, 1)
-        quantise_a(3, 0, G)
+        for h in range(2):
+            weigh("far", last - 1, h)
 
-        runs = {
-            2: [("f", 4), ("n", 0)],
-            3: [("f", 5), ("n", 1)],
-            4: [("n", 2), ("n", 3)],
-            5: [("n", 4), ("n", 5)],
-            6: [("n", 6), ("n", 7)],
-            7: [],
-        }
-        for i in range(2, ROW_TILES):
-            for key in runs[i]:
-                transpose_tile(key)
-            weigh("mid", i - 1, 1)
-            for kind, n in runs[i]:
-                if kind == "n":
-                    interleave_near(n)
-            for kind, n in runs[i + 1]:
-                presort((kind, n), frames_raw[n] if kind == "f" else near_raw[n])
-            product("far", i, 0)
-            product("far", i, 1)
-            product("mid", i, 0)
-            first_kind, first = runs[i][0]
-            if first_kind == "f":
-                divide(first, 0, 2)
-                divide(first, 2, 4)
-                weigh("far", i, 0)
-                quantise_a(first, 0, G)
-            else:
-                weigh("far", i, 0)
-                quantise_near(first)
-            weigh("far", i, 1)
-            quantise_near(runs[i][1][1])
+        def near_run(pair):
+            for n in (2 * pair, 2 * pair + 1):
+                transpose_tile(("n", n))
+                for b in range(2):
+                    interleave_near(n, b)
+            for n in (2 * pair + 3, 2 * pair + 4):
+                if n < 6:
+                    presort(("n", n))
+            if pair < 2:
+                presort_quadrants(pair)
+
+        near_run(0)
+        for h in range(2):
+            product("far", last, h)
+        for i in (3, 2, 1):
+            weigh_parked(i, 0)
+        weigh("far", last, 0)
+        quantise_near(0)
+        weigh("far", last, 1)
+        weigh_parked(0, 0)
+
+        for i in range(ROW_TILES):
+            if i == 3:
+                near_run(1)
+            if i > 0:
+                product("mid", i, 0)
+                weigh("mid", i, 0)
+            join(i, 0)
+            if i == 2:
+                turn_quadrants(0)
+        turn_quadrants(1)
+        near_run(2)
+        widen_ring()
+        quantise_near(1)
+        for b in range(2):
+            interleave_turned(b)
+        for i in range(ROW_TILES):
             product("mid", i, 1)
-            weigh("mid", i, 0)
+            weigh("mid", i, 1)
+            if i == 0:
+                quantise_near(2)
+            if i == 1:
+                for k in (3, 2, 1):
+                    weigh_parked(k, 1)
+            if i == 2:
+                quantise_near(3)
+                weigh_parked(0, 1)
+        for i in range(ROW_TILES):
+            join(i, 1)
 
-        for key in runs[6]:
-            transpose_tile(key)
-        weigh("mid", ROW_TILES - 1, 1)
-        interleave_near(6)
-        interleave_near(7)
         order = [(i, h) for h in range(2) for i in range(ROW_TILES)]
-        for k, (i, h) in enumerate(order[:-1]):
+        for i, h in order[:-1]:
             product("near", i, h)
             finish(i, h)
-            if k < 2:
-                quantise_near(6 + k)
         for part in range(len(LAST_PARTS)):
             product("near", ROW_TILES - 1, 1, part=part)
         for part in range(len(LAST_PARTS)):

from contextlib import ExitStack

import concourse.mybir as mybir
from concourse.masks import make_identity

D, T, N = 768, 2048, 1024
FLOPS = 3 * 2 * D * T * N

F32 = mybir.dt.float32
BF16 = mybir.dt.bfloat16
I32 = mybir.dt.int32
U32 = mybir.dt.uint32
U8 = mybir.dt.uint8
FP8X4 = mybir.dt.float8_e4m3fn_x4
FP4X4 = mybir.dt.float4_e2m1fn_x4
ALU = mybir.AluOpType

P = 128
G = T // 512
ROW_TILES = D // P
NEAR_TILES = N // P
HALF = 512
LAST_PARTS = [(0, 256), (256, 128), (384, 128)]


def tile_wpe_tied_tap_correlation_s10_kernel(
    tc, frames, variance, near, mid_words, mid_scales, far_words, far_scales, decay_mid, decay_far, out
):
    nc = tc.nc
    with ExitStack() as ctx:
        keep = ctx.enter_context(tc.tile_pool(name="keep", bufs=1))
        stage = ctx.enter_context(tc.tile_pool(name="stage", bufs=2))
        psum = ctx.enter_context(tc.psum_pool(name="psum", bufs=1))
        ctx.enter_context(tc.manual_schedule())

        ident = keep.tile([P, P], F32, name="ident")
        make_identity(nc, ident[:])

        far_plane = keep.tile([P, G, N], U8, name="far_plane", align_bytes=64)
        mid_plane = keep.tile([P, N], U8, name="mid_plane", align_bytes=64)
        warm_in = keep.tile([P, 4 * P], BF16, name="warm_in", align_bytes=64)
        warm_codes = keep.tile([P, P], U32, name="warm_codes", align_bytes=64)
        warm_scales = keep.tile([P, P], U8, name="warm_scales", align_bytes=64)
        nc.vector.memset(warm_in[:], 0.0)
        nc.vector.memset(mid_plane[:].bitcast(I32), 0)
        nc.vector.quantize_mx(out=warm_codes[:].bitcast(FP8X4), scales=warm_scales[:], in_=warm_in[:])
        nc.vector.memset(far_plane[:].rearrange("p g n -> p (g n)").bitcast(I32), 0)

        var_sb = keep.tile([P, G, 4], BF16, name="var_sb")
        inv_var = keep.tile([P, G, 4], F32, name="inv_var")
        raw_words = {}
        quadrant_words = {}
        far_codes = {}
        mid_codes = {}
        decay_raw = {}

        def load_frames(i, parts, only=None):
            width = T // parts
            for c in range(parts) if only is None else [only]:
                raw = keep.tile([P, width], BF16, name="frames_%d_%d" % (i, c), align_bytes=64)
                nc.sync.dma_start(out=raw[:], in_=frames[i * P : (i + 1) * P, c * width : (c + 1) * width])
                raw_words["f", i, c] = raw[:].bitcast(F32)

        def load_near(n):
            raw = keep.tile([P, T], BF16, name="near_%d" % n, align_bytes=64)
            nc.sync.dma_start(out=raw[:], in_=near[n * P : (n + 1) * P, :])
            raw_words["n", n, 0] = raw[:].bitcast(F32)

        def load_near_by_quadrant(b):
            raw = keep.tile([P, 2, 8, P], BF16, name="near_last_%d" % b, align_bytes=64)
            rows = near[N - 2 * P :, :].rearrange("(s r) (g q k) -> g q r s k", r=32, g=G, q=4)
            for gg in range(2):
                for q in (0, 2, 1, 3):
                    nc.sync.dma_start(out=raw[32 * q : 32 * (q + 1), gg], in_=rows[2 * b + gg, q])
            quadrant_words[b] = raw[:].rearrange("r g s k -> r (g s k)").bitcast(F32)

        def load_far(g):
            codes = keep.tile([P, 2 * N], U8, name="far_%d" % g, align_bytes=64)
            nc.sync.dma_start(out=codes[:].bitcast(I32), in_=far_words[g].bitcast(I32))
            far_codes[g] = codes

        def load_mid(h):
            codes = keep.tile([P, G, HALF], U32, name="mid_%d" % h, align_bytes=64)
            src = mid_words.rearrange("g p n t -> p g (n t)")[:, :, 4 * HALF * h : 4 * HALF * (h + 1)]
            nc.sync.dma_start(out=codes[:].bitcast(I32), in_=src.bitcast(I32))
            mid_codes[h] = codes

        def load_far_scales(which, queue):
            rows = far_scales.rearrange("g (q r) n -> r q g n", r=4)
            engine = nc.sync if queue == "sync" else nc.gpsimd
            for r in which:
                engine.dma_start(out=far_plane[r:P:32, :, :].bitcast(I32), in_=rows[r].bitcast(I32))

        def load_mid_scales():
            for q in range(4):
                nc.sync.dma_start(
                    out=mid_plane[32 * q : 32 * q + 16, :].bitcast(I32),
                    in_=mid_scales[:, 4 * q : 4 * q + 4, :].bitcast(I32),
                )

        def load_decay(which, vec):
            raw = keep.tile([P, 8], BF16, name="decay_raw_" + which)
            nc.sync.dma_start(out=raw[:], in_=vec.rearrange("(p c) -> p c", p=P))
            decay_raw[which] = raw

        def load_variance():
            nc.sync.dma_start(out=var_sb[:], in_=variance.rearrange("(g p t) -> p g t", g=G, p=P))

        load_variance()
        load_frames(0, 2, 0)
        load_decay("far", decay_far)
        load_decay("mid", decay_mid)
        load_frames(0, 2, 1)
        load_frames(1, 2)
        load_far_scales((0, 1, 2, 3), "sync")
        for g in range(G):
            load_far(g)
        load_frames(2, 2)
        for i in range(3, ROW_TILES):
            load_frames(i, 1)
        load_near(0)
        load_near(1)
        load_mid_scales()
        load_mid(0)
        load_near(2)
        load_near(3)
        load_near(4)
        load_near_by_quadrant(0)
        load_near(5)
        load_near_by_quadrant(1)
        load_mid(1)

        nc.vector.reciprocal(out=inv_var[:], in_=var_sb[:])

        rings = {"tp": ["tp0", "tp1", "tp2", "tp3"], "acc": ["acc0", "acc1", "acc2", "acc3"]}
        taken = []

        def bank(kind, shape):
            tag = rings[kind][0]
            rings[kind] = rings[kind][1:] + [tag]
            taken.append(tag)
            return psum.tile(shape, F32, name="bank_%d" % len(taken), tag=tag)

        def widen_ring():
            rings["acc"] = rings["acc"] + rings["tp"]

        sorted_words = {}

        def presort(key, half=None):
            passes = G if half is None else G // 2
            raw = raw_words[key[0], key[1], 0 if half is None else half]
            if half is None:
                srt = stage.tile([P, G, 2, P], F32, name="sorted_%s_%d" % key, tag="sorted", bufs=5, align_bytes=64)
            else:
                srt = keep.tile([P, passes, 2, P], F32, name="sorted_%s_%d_%d" % (key + (half,)), align_bytes=64)
            nc.scalar.copy(
                out=srt[:].rearrange("r g u (c i) -> r g c u i", i=4),
                in_=raw.rearrange("r (g c i u) -> r g c u i", g=passes, i=4, u=2),
            )
            for g in range(passes):
                sorted_words[key, g + (0 if half is None else passes * half)] = srt[:, g]

        banks = {}

        def transpose_bank(key, b):
            tp = bank("tp", [P, 2, 2, P])
            for gg in range(2):
                for u in range(2):
                    if (key, 2 * b + gg) in sorted_words:
                        src = sorted_words[key, 2 * b + gg][:, u, :]
                    else:
                        src = raw_words[key[0], key[1], b][:, 256 * gg + u : 256 * (gg + 1) : 2]
                    nc.tensor.transpose(tp[:, u, gg, :], src, ident[:])
            banks[key, b] = tp

        def transpose_tile(key):
            for b in range(2):
                transpose_bank(key, b)

        decay_b = {}

        def spread_decay(which):
            tp = bank("acc", [P, 4, P])
            words = decay_raw[which][:].bitcast(F32)
            for c in range(4):
                nc.tensor.transpose(tp[:, c, :], words[:, c : c + 1].to_broadcast([P, P]), ident[:])
            banks["decay", which] = tp

        def keep_decay(which):
            wide = keep.tile([P, N], BF16, name="decay_" + which, align_bytes=64)
            nc.scalar.copy(
                out=wide[:].bitcast(F32).rearrange("m (p c) -> m p c", c=4),
                in_=banks["decay", which][:].rearrange("m c p -> m p c"),
            )
            decay_b[which] = wide

        a_grouped = {}
        a_codes = {}
        a_scales = {}

        def divide(i, g, g1=None):
            g1 = g + 1 if g1 is None else g1
            if g == 0:
                a_grouped[i] = stage.tile([P, G, P, 4], BF16, name="a_grouped_%d" % i, tag="a_grouped", align_bytes=64)
                a_codes[i] = keep.tile([P, G, P], U32, name="a_codes_%d" % i, align_bytes=64)
                a_scales[i] = keep.tile([P, G, P], U8, name="a_scales_%d" % i, align_bytes=64)
            tp = banks[("f", i), g // 2]
            pairs = tp[:].rearrange("p u g r -> p (u g r)").bitcast(BF16)
            pairs = pairs.rearrange("p (u g r e) -> p g r u e", g=2, u=2, e=2)[:, g % 2 : g % 2 + g1 - g]
            factors = inv_var[:, g:g1, :].rearrange("p g (u e) -> p g u e", u=2).unsqueeze(2)
            nc.vector.tensor_tensor(
                out=a_grouped[i][:, g:g1].rearrange("p g r (u e) -> p g r u e", u=2),
                in0=pairs,
                in1=factors.to_broadcast([P, g1 - g, P, 2, 2]),
                op=ALU.mult,
            )

        def quantise_a(i, g0, g1):
            nc.vector.quantize_mx(
                out=a_codes[i][:, g0:g1, :].rearrange("p g r -> p (g r)").bitcast(FP8X4),
                scales=a_scales[i][:, g0:g1, :].rearrange("p g r -> p (g r)"),
                in_=a_grouped[i][:, g0:g1].rearrange("p g r t -> p (g r t)"),
            )

        near_grouped = {}
        near_codes = {}
        near_scales = {}
        for h in range(2):
            near_codes[h] = keep.tile([P, G, HALF], U32, name="near_codes_%d" % h, align_bytes=64)
            near_scales[h] = keep.tile([P, G, HALF], U8, name="near_scales_%d" % h, align_bytes=64)

        def interleave_near(n, b, engine="scalar"):
            if n % 2 == 0 and b == 0:
                near_grouped[n // 2] = stage.tile(
                    [P, G, 2 * P, 4], BF16, name="n_grouped_%d" % (n // 2), tag="n_grouped", align_bytes=64
                )
            words = near_grouped[n // 2][:].rearrange("p g r t -> p (g r t)").bitcast(F32)
            words = words.rearrange("p (g r u) -> p g r u", g=G, u=2)
            dst = words[:, 2 * b : 2 * b + 2, (n % 2) * P : (n % 2 + 1) * P]
            src = banks[("n", n), b][:].rearrange("p u g r -> p g r u")
            if engine == "scalar":
                nc.scalar.copy(out=dst, in_=src)
            else:
                nc.vector.tensor_copy(out=dst, in_=src)

        turned = {}

        def presort_quadrants(b):
            srt = stage.tile([P, 16, 2, 32], F32, name="sorted_last_%d" % b, tag="sorted", bufs=5, align_bytes=64)
            nc.scalar.copy(
                out=srt[:].rearrange("r s u (c i) -> r s c u i", i=4),
                in_=quadrant_words[b].rearrange("r (s c i u) -> r s c u i", s=16, i=4, u=2),
            )
            sorted_words["last", b] = srt

        def turn_quadrants(b):
            turned[b] = keep.tile([P, 16, 2, 32], F32, name="turned_%d" % b, align_bytes=64)
            nc.vector.transpose(
                out=turned[b][:].rearrange("p s u r -> p (s u r)"),
                in_=sorted_words["last", b][:].rearrange("r s u j -> r (s u j)"),
            )

        def interleave_turned(b):
            if b == 0:
                near_grouped[3] = stage.tile([P, G, 2 * P, 4], BF16, name="n_grouped_3", tag="n_grouped", align_bytes=64)
            words = near_grouped[3][:, 2 * b : 2 * b + 2].rearrange("p g r t -> p (g r t)").bitcast(F32)
            nc.scalar.copy(
                out=words.rearrange("p (s r u) -> p s r u", s=16, u=2),
                in_=turned[b][:].rearrange("p s u r -> p s r u"),
            )

        def quantise_near(pair):
            h, cols = pair // 2, slice((pair % 2) * 2 * P, (pair % 2 + 1) * 2 * P)
            for g in range(G):
                nc.vector.quantize_mx(
                    out=near_codes[h][:, g, cols].bitcast(FP8X4),
                    scales=near_scales[h][:, g, cols],
                    in_=near_grouped[pair][:, g].rearrange("p r t -> p (r t)"),
                )

        accs = {}

        def product(kind, i, h, g0=0, g1=G, part=None):
            lo, width = (0, HALF) if part is None else LAST_PARTS[part]
            key = (kind, i, h) if part is None else (kind, i, h, part)
            if g0 == 0:
                accs[key] = bank("acc", [P, width])
            acc = accs[key]
            cols = slice(h * HALF, (h + 1) * HALF)
            for g in range(g0, g1):
                if kind == "far":
                    words = far_codes[g][:, 2 * h * HALF : 2 * (h + 1) * HALF]
                    rhs, rhs_scale = words.bitcast(FP4X4), far_plane[:, g, cols]
                elif kind == "mid":
                    rhs, rhs_scale = mid_codes[h][:, g, :].bitcast(FP8X4), mid_plane[4 * g : P, cols]
                else:
                    rhs = near_codes[h][:, g, lo : lo + width].bitcast(FP8X4)
                    rhs_scale = near_scales[h][:, g, lo : lo + width]
                nc.tensor.matmul_mx(
                    out=acc[:],
                    lhsT=a_codes[i][:, g, :].bitcast(FP8X4),
                    lhsT_scale=a_scales[i][:, g, :],
                    rhs=rhs,
                    rhs_scale=rhs_scale,
                    start=(g == 0),
                    stop=(g == G - 1),
                )

        warm_bank = bank("acc", [P, 4, P])

        def warm_up(count):
            for k in range(count):
                nc.tensor.matmul_mx(
                    out=warm_bank[:, k % 4, :],
                    lhsT=warm_codes[:].bitcast(FP8X4),
                    lhsT_scale=warm_scales[:],
                    rhs=warm_codes[:].bitcast(FP8X4),
                    rhs_scale=warm_scales[:],
                    start=True,
                    stop=True,
                )

        tied = {}

        def weigh(kind, i, h):
            part = keep.tile([P, HALF], F32, name="tied_%s_%d_%d" % (kind, i, h))
            nc.vector.tensor_tensor(
                out=part[:], in0=accs[kind, i, h][:], in1=decay_b[kind][:, h * HALF : (h + 1) * HALF], op=ALU.mult
            )
            tied[kind, i, h] = part

        def park(i, h):
            part = keep.tile([P, HALF], F32, name="tied_far_%d_%d" % (i, h))
            nc.scalar.copy(out=part[:], in_=accs["far", i, h][:])
            tied["far", i, h] = part

        def weigh_parked(i, h):
            part = tied["far", i, h]
            nc.vector.tensor_tensor(
                out=part[:], in0=part[:], in1=decay_b["far"][:, h * HALF : (h + 1) * HALF], op=ALU.mult
            )

        def join(i, h):
            nc.gpsimd.tensor_tensor(
                out=tied["far", i, h][:], in0=tied["far", i, h][:], in1=tied["mid", i, h][:], op=ALU.add
            )

        def finish(i, h, part=None):
            lo, width = (0, HALF) if part is None else LAST_PARTS[part]
            key = ("near", i, h) if part is None else ("near", i, h, part)
            result = tied["mid", i, h][:, lo : lo + width]
            nc.vector.tensor_tensor(out=result, in0=accs[key][:], in1=tied["far", i, h][:, lo : lo + width], op=ALU.add)
            nc.sync.dma_start(out=out[i * P : (i + 1) * P, h * HALF + lo : h * HALF + lo + width], in_=result)

        warm_up(15)
        transpose_tile(("f", 0))
        warm_up(12)
        spread_decay("far")
        spread_decay("mid")
        for b in range(2):
            presort(("f", 1), b)
            transpose_bank(("f", 1), b)
        keep_decay("far")
        keep_decay("mid")
        for b in range(2):
            presort(("f", 2), b)
        early = [(i, g) for i in range(2) for g in range(G)]
        divide(0, 0, 1)
        for k, (i, g) in enumerate(early):
            if k + 1 < len(early):
                divide(early[k + 1][0], early[k + 1][1], early[k + 1][1] + 1)
            quantise_a(i, g, g + 1)
            if (i, g) == (1, 1):
                transpose_tile(("f", 2))
            for h in range(2):
                product("far", i, h, g, g + 1)
        park(0, 0)
        presort(("f", 3))
        park(0, 1)

        runs = {2: [3], 3: [4, 5], 4: []}
        upcoming = {2: [], 3: [("n", 0)], 4: [("n", 1), ("n", 2)]}
        for i in range(2, ROW_TILES - 1):
            divide(i, 0, 2)
            divide(i, 2, 4)
            quantise_a(i, 0, 2)
            quantise_a(i, 2, 4)
            for n in runs[i]:
                transpose_tile(("f", n))
            if i == 2:
                presort(("f", 4))
                presort(("f", 5))
            for h in range(2):
                park(i - 1, h)
            for key in upcoming[i]:
                presort(key)
            if i == 4:
                product("mid", 0, 0)
            for h in range(2):
                product("far", i, h)
        last = ROW_TILES - 1
        divide(last, 0, 2)
        divide(last, 2, 4)
        quantise_a(last, 0, 2)
        quantise_a(last, 2, 4)
        weigh("mid", 0, 0)
        for h in range(2):
            weigh("far", last - 1, h)

        def near_run(pair):
            for n in (2 * pair, 2 * pair + 1):
                transpose_tile(("n", n))
                for b in range(2):
                    interleave_near(n, b)
            for n in (2 * pair + 3, 2 * pair + 4):
                if n < 6:
                    presort(("n", n))
            if pair < 2:
                presort_quadrants(pair)

        near_run(0)
        for h in range(2):
            product("far", last, h)
        for i in (3, 2, 1):
            weigh_parked(i, 0)
        weigh("far", last, 0)
        quantise_near(0)
        weigh("far", last, 1)
        weigh_parked(0, 0)

        for i in range(ROW_TILES):
            if i == 3:
                near_run(1)
            if i > 0:
                product("mid", i, 0)
                weigh("mid", i, 0)
            join(i, 0)
            if i == 2:
                turn_quadrants(0)
        turn_quadrants(1)
        near_run(2)
        widen_ring()
        quantise_near(1)
        for b in range(2):
            interleave_turned(b)
        for i in range(ROW_TILES):
            product("mid", i, 1)
            weigh("mid", i, 1)
            if i == 0:
                quantise_near(2)
            if i == 1:
                for k in (3, 2, 1):
                    weigh_parked(k, 1)
            if i == 2:
                quantise_near(3)
                weigh_parked(0, 1)
        for i in range(ROW_TILES):
            join(i, 1)

        order = [(i, h) for h in range(2) for i in range(ROW_TILES)]
        for i, h in order[:-1]:
            product("near", i, h)
            finish(i, h)
        for part in range(len(LAST_PARTS)):
            product("near", ROW_TILES - 1, 1, part=part)
        for part in range(len(LAST_PARTS)):
            finish(ROW_TILES - 1, 1, part)
